import numpy as np
import ml_dtypes


def mxq(x, axis, fmt="e4m3"):
    dtype, down = {"e4m3": (ml_dtypes.float8_e4m3fn, 7), "e5m2": (ml_dtypes.float8_e5m2, 14)}[fmt]
    v = np.moveaxis(np.asarray(x, np.float32).astype(ml_dtypes.bfloat16).astype(np.float64), axis, -1)
    blocks = v.reshape(v.shape[:-1] + (-1, 32))
    amax = np.abs(blocks).max(-1, keepdims=True)
    byte = np.maximum(np.where(amax > 0, np.frexp(amax)[1] - 1 + 127, 0) - down, 1)
    scale = np.exp2(byte - 127.0)
    codes = (blocks / scale).astype(np.float32).astype(dtype).astype(np.float64)
    return np.moveaxis((codes * scale).reshape(v.shape), -1, axis)


WIDE = False


def mx_kscale(k):
    if not WIDE:
        return np.ones(k)
    levels = np.array([10, -10, 5, -5, 0])
    if k % 512:
        return np.exp2(np.random.permutation(np.resize(levels, k // 32))).repeat(32)
    a = np.empty((k // 512, 16))
    for p in range(k // 512):
        a[p, :8] = np.random.permutation(np.resize(levels, 8))
        for g in range(8):
            far = levels[np.abs(levels - a[p, g]) >= 10]
            a[p, g + 8] = far[np.random.randint(len(far))]
    return np.exp2(a.ravel()).repeat(32)


def f64(x):
    return np.asarray(x).astype(np.float64)


def striped8(idx):
    return np.concatenate([x.reshape(-1, 16).T for x in idx]).astype(np.uint16)


def runs(offs, k):
    lists = np.stack([offs[16 * r : 16 * r + 16].T.reshape(-1) for r in range(8)]).astype(np.int64)
    return lists[np.arange(k) % 512 // 64]


def pack_weight(w):
    k, n = w.shape
    w = f64(np.asarray(w, np.float32).astype(ml_dtypes.bfloat16)).reshape(k // 32, 32, n)
    amax = np.abs(w).max(1)
    byte = np.clip(np.where(amax > 0, np.frexp(amax)[1] - 1 + 127 - 7, 1), 1, 254)
    scaled = (w * np.exp2(127.0 - byte)[:, None, :]).reshape(k, n).astype(np.float32)
    words = np.ascontiguousarray(scaled.reshape(k // 512, 128, 4, n).transpose(0, 1, 3, 2)).astype(ml_dtypes.float8_e4m3fn).view(np.uint8)
    return words, np.ascontiguousarray(byte.astype(np.uint8).reshape(k // 512, 16, n))


def unpack_weight(words, scales):
    g, p, n, _ = words.shape
    vals = np.ascontiguousarray(words).view(ml_dtypes.float8_e4m3fn).astype(np.float64) * np.repeat(np.exp2(scales.astype(np.float64) - 127.0), 8, axis=1)[..., None]
    return vals.transpose(0, 1, 3, 2).reshape(g * 512, n)


def sigmoid(v):
    return 1.0 / (1.0 + np.exp(-np.maximum(v, -700.0)))

def planes(y):
    n, m = y.shape
    v = y.astype(np.float32).astype(ml_dtypes.bfloat16).astype(np.float64).reshape(n // 32, 32, m)
    top = np.abs(v).max(1)
    byte = np.clip(np.where(top > 0, np.frexp(top)[1] - 1 + 127 - 7, 1), 1, 254)
    codes = (v * np.exp2(127.0 - byte)[:, None, :]).reshape(n, m).astype(np.float32).astype(ml_dtypes.float8_e4m3fn).view(np.uint8)
    words = codes.reshape(n // 512, 128, 4, m).transpose(0, 1, 3, 2)
    return np.ascontiguousarray(words), np.ascontiguousarray(byte.astype(np.uint8).reshape(n // 512, 16, m))


K, T, S, N, H = 512, 2048, 512, 512, 512


def setup_inputs():
    n = np.random.standard_normal
    s = mx_kscale(K)[:, None]
    u = mx_kscale(H)
    packed_xT = pack_weight(n((K, T)) * s)
    packed_w1 = pack_weight(n((K, H)) / np.sqrt(K) / s)
    packed_w2 = pack_weight(n((H, N)) / np.sqrt(H) / u[:, None])
    return {
        "x_words": packed_xT[0],
        "x_scales": packed_xT[1],
        "w1_words": packed_w1[0],
        "w1_scales": packed_w1[1],
        "gn": (np.random.uniform(0.5, 1.5, (H, 1)) * u[:, None]).astype(np.float32),
        "w2_words": packed_w2[0],
        "w2_scales": packed_w2[1],
        "offs": striped8(np.random.randint(0, T, (8, S))),
        "n1": striped8(np.stack([np.random.permutation(S) for _ in range(8)])),
        "n2": striped8(np.stack([np.random.permutation(S) for _ in range(8)])),
        "n3": striped8(np.stack([np.random.permutation(S) for _ in range(8)])),
    }


def reference(x_words, x_scales, w1_words, w1_scales, gn, w2_words, w2_scales, offs, n1, n2, n3):
    xq = unpack_weight(x_words, x_scales)[np.arange(K)[:, None], runs(offs, K)]
    y = unpack_weight(w1_words, w1_scales).T @ xq
    st = y[np.arange(H)[:, None], runs(n1, H)] - y
    z = f64(gn) * (y * (sigmoid(st[np.arange(H)[:, None], runs(n2, H)])))
    h = unpack_weight(w2_words, w2_scales).T @ mxq(z, 0, "e4m3")
    pa = h[np.arange(N)[:, None], runs(n3, N)]
    out_0 = (2.0 * (h * pa)) / ((h) ** 2 + (pa) ** 2 + 0.5)
    return (out_0,) + planes(out_0)

@@ -1,0 +1,266 @@
+from contextlib import ExitStack
+
+import concourse.mybir as mybir
+
+K, T, S, N, H = 512, 2048, 512, 512, 512
+FLOPS = 2 * K * H * S + 2 * H * N * S
+
+F32 = mybir.dt.float32
+BF16 = mybir.dt.bfloat16
+I32 = mybir.dt.int32
+U32 = mybir.dt.uint32
+U16 = mybir.dt.uint16
+U8 = mybir.dt.uint8
+FP8X4 = mybir.dt.float8_e4m3fn_x4
+ACT = mybir.ActivationFunctionType
+ALU = mybir.AluOpType
+
+P = 128
+PACK = 4
+HALF = S // 2
+CHUNK = S // 4
+A_ACT = ((2, 0), (2, 1))
+B_ACT = ((2, 0), (3, 0), (3, 1))
+HH_DVE = ((0, 0), (1, 0))
+C_DVE = ((0, 1), (1, 1))
+Y_DVE = ((0, 0), (1, 0))
+IL_ACT = (1, 2)
+PIECES = ((0, 128), (128, 128), (256, 128), (384, 128))
+
+
+def entries(lst, start, count):
+    return lst[:, start // 16 : (start + count) // 16]
+
+
+def tile_picked_hashhopdharm_none_po_kernel(
+    tc, x_words, x_scales, w1_words, w1_scales, gn, w2_words, w2_scales, offs, n1, n2, n3, out_0, out_1, out_2
+):
+    nc = tc.nc
+    with ExitStack() as ctx:
+        lists = ctx.enter_context(tc.tile_pool(name="lists", bufs=1))
+        sb = ctx.enter_context(tc.tile_pool(name="sb", bufs=1))
+        early = ctx.enter_context(tc.tile_pool(name="early", bufs=1))
+        ps = ctx.enter_context(tc.psum_pool(name="ps", bufs=1))
+
+        def words_of(dram):
+            return dram[0].rearrange("p c r -> p (c r)").bitcast(I32)
+
+        l_offs = lists.tile([P, S // 16], U16, name="l_offs")
+        l_n1 = lists.tile([P, S // 16], U16, name="l_n1")
+        l_n2 = lists.tile([P, S // 16], U16, name="l_n2")
+        l_n3 = lists.tile([P, S // 16], U16, name="l_n3")
+        for tile, dram in ((l_offs, offs), (l_n1, n1), (l_n2, n2), (l_n3, n3)):
+            nc.sync.dma_start(tile[:], dram)
+
+        table_bytes = sb.tile([P, T], U8, name="table_bytes", tag="x_side", align_bytes=64)
+        w_raw_bytes = sb.tile([P, H], U8, name="w_raw_bytes", align_bytes=64)
+        x_plane = sb.tile([P, S], U8, name="x_plane", align_bytes=64)
+        for tile in (table_bytes, w_raw_bytes, x_plane):
+            nc.vector.memset(tile[:].bitcast(I32), 0)
+
+        x_rows = x_scales[0].rearrange("(m e) c -> e m c", e=2)
+        for e in range(2):
+            nc.scalar.dma_start(table_bytes[e:P:16, :].bitcast(I32), x_rows[e].bitcast(I32))
+
+        table_words = early.tile([P, T], U32, name="table_words", align_bytes=64, offset=0)
+        nc.sync.dma_start(table_words[:].bitcast(I32), words_of(x_words))
+        w1_raw_words = sb.tile([P, H], U32, name="w1_raw_words", align_bytes=64)
+        nc.sync.dma_start(w1_raw_words[:].bitcast(I32), words_of(w1_words))
+
+        def load_plane(queues, dram):
+            for q in range(4):
+                queues[q // 2].dma_start(w_raw_bytes[32 * q : 32 * q + 4, :].bitcast(I32), dram[0, 4 * q : 4 * q + 4, :].bitcast(I32))
+
+        load_plane((nc.scalar, nc.gpsimd), w1_scales)
+        gain = sb.tile([P, PACK], F32, name="gain")
+        nc.gpsimd.dma_start(gain[:], gn.rearrange("(p t) o -> p (t o)", t=PACK))
+
+        picked_bytes = sb.tile([P, S], U8, name="picked_bytes", align_bytes=64)
+        nc.vector.tensor_copy(picked_bytes[:], table_bytes[:].indirect(l_offs[:]))
+        for e in range(2):
+            nc.sync.dma_start(x_plane[2 + e : P : 32, :].bitcast(I32), picked_bytes[16 + e : P : 32, :].bitcast(I32))
+        for q in range(4):
+            rows = slice(32 * q, 32 * q + 2)
+            nc.vector.tensor_copy(x_plane[rows, :].bitcast(I32), picked_bytes[rows, :].bitcast(I32))
+
+        def deal(copy, dealt, raw):
+            copy(dealt[:].rearrange("p (t m) -> p m t", t=PACK), raw[:].rearrange("p (m t) -> p m t", t=PACK))
+
+        w1_plane = [early.tile([P, P], U8, name=f"w1_plane{t}", align_bytes=64, offset=P * t) for t in range(PACK)]
+        w1_codes = sb.tile([P, H], U32, name="w1_codes", align_bytes=64)
+        deal(nc.scalar.copy, w1_codes, w1_raw_words)
+        x_codes = sb.tile([P, S], U32, name="x_codes", tag="x_side", align_bytes=64)
+        nc.vector.tensor_copy(x_codes[:], table_words[:].indirect(l_offs[:]))
+        for t in range(PACK):
+            nc.vector.tensor_copy(w1_plane[t][:], w_raw_bytes[:, t:H:PACK])
+        w2_raw_words = early.tile([P, N], U32, name="w2_raw_words", align_bytes=64, offset=H)
+        nc.sync.dma_start(w2_raw_words[:].bitcast(I32), words_of(w2_words))
+        load_plane((nc.sync, nc.sync), w2_scales)
+
+        halves = [slice(h * HALF, (h + 1) * HALF) for h in range(2)]
+        y_bank = [[ps.tile([P, HALF], F32, name=f"y_bank{t}_{h}", tag=f"bank{t}_{h}") for h in range(2)] for t in range(PACK)]
+        y = [sb.tile([P, S], F32, name=f"y{t}") for t in range(PACK)]
+        y_n1 = [sb.tile([P, S], F32, name=f"y_n1_{t}", tag=f"y_n1_{t}", align_bytes=64) for t in range(PACK)]
+        st = [sb.tile([P, S], F32, name=f"st{t}", tag=f"st{t}", align_bytes=64) for t in range(PACK)]
+        sig = [[sb.tile([P, HALF], F32, name=f"sig{t}_{h}") for h in range(2)] for t in range(PACK)]
+        z = [sb.tile([P, PACK, HALF], BF16, name=f"z{h}") for h in range(2)]
+        for t in range(PACK):
+            for h in range(2):
+                nc.tensor.matmul_mx(
+                    out=y_bank[t][h][:], lhsT=w1_codes[:, P * t : P * (t + 1)].bitcast(FP8X4), lhsT_scale=w1_plane[t][:],
+                    rhs=x_codes[:, halves[h]].bitcast(FP8X4), rhs_scale=x_plane[:, halves[h]], start=True, stop=True,
+                )
+
+        def fetch(on_scalar, out, window, offsets):
+            if on_scalar:
+                nc.scalar.activation(out=out, in_=window[:].indirect(offsets), func=ACT.Copy)
+            else:
+                nc.vector.tensor_copy(out, window[:].indirect(offsets))
+
+        for t in range(PACK):
+            for h in range(2):
+                copy = nc.vector.tensor_copy if (t, h) in Y_DVE else nc.scalar.copy
+                copy(y[t][:, halves[h]], y_bank[t][h][:])
+        for t in range(PACK):
+            for h in range(2):
+                fetch((t, h) in A_ACT, y_n1[t][:, halves[h]], y[t], entries(l_n1, h * HALF, HALF))
+            for h in range(2):
+                nc.vector.tensor_tensor(st[t][:, halves[h]], y_n1[t][:, halves[h]], y_bank[t][h][:], ALU.subtract)
+        for t in range(PACK):
+            for h in range(2):
+                nc.scalar.activation(out=sig[t][h][:], in_=st[t][:].indirect(entries(l_n2, h * HALF, HALF)), func=ACT.Sigmoid)
+        w2_plane = sb.tile([P, N], U8, name="w2_plane", tag="y_n1_1", align_bytes=64)
+        w2_codes = sb.tile([P, N], U32, name="w2_codes", tag="st3", align_bytes=64)
+        deal(nc.scalar.copy, w2_codes, w2_raw_words)
+        deal(nc.vector.tensor_copy, w2_plane, w_raw_bytes)
+
+        def interleave(copy, grouped, planes):
+            copy(grouped[:].rearrange("p (c i t) -> p c t i", i=4, t=PACK), planes.rearrange("p t (c i) -> p c t i", i=4))
+
+        def make_z(h):
+            for t in range(PACK):
+                nc.vector.scalar_tensor_tensor(
+                    out=z[h][:, t, :], in0=y_bank[t][h][:], scalar=gain[:, t : t + 1],
+                    in1=sig[t][h][:], op0=ALU.mult, op1=ALU.mult,
+                )
+
+        def group_z(h, start, width):
+            grouped = sb.tile([P, PACK * width], BF16, name=f"z_grouped{h}_{start}", align_bytes=64)
+            interleave(nc.vector.tensor_copy, grouped, z[h][:, :, start : start + width])
+            return grouped
+
+        def second_product(banks, grouped, h, start, width):
+            codes = sb.tile([P, width], U32, name=f"z_codes{h}_{start}", align_bytes=64)
+            plane = sb.tile([P, width], U8, name=f"z_plane{h}_{start}", align_bytes=64)
+            nc.vector.quantize_mx(out=codes[:].bitcast(FP8X4), scales=plane[:], in_=grouped[:])
+            for t in range(PACK):
+                cols = slice(P * t, P * (t + 1))
+                nc.tensor.matmul_mx(
+                    out=banks[t][:, start : start + width], lhsT=w2_codes[:, cols].bitcast(FP8X4), lhsT_scale=w2_plane[:, cols],
+                    rhs=codes[:].bitcast(FP8X4), rhs_scale=plane[:], start=True, stop=True,
+                )
+
+        hw = [sb.tile([P, S], F32, name=f"h{t}") for t in range(PACK)]
+        hh = [sb.tile([P, PACK, HALF], F32, name=f"hh{h}") for h in range(2)]
+        h_first = [ps.tile([P, HALF], F32, name=f"h_first{t}", tag=f"bank{t}_0") for t in range(PACK)]
+        make_z(0)
+        second_product(h_first, group_z(0, 0, HALF), 0, 0, HALF)
+        make_z(1)
+        h_second = [ps.tile([P, HALF], F32, name=f"h_second{t}", tag=f"bank{t}_1") for t in range(PACK)]
+        z_last = [group_z(1, start, CHUNK) for start in (0, CHUNK)]
+        second_product(h_second, z_last[0], 1, 0, CHUNK)
+        second_product(h_second, z_last[1], 1, CHUNK, CHUNK)
+        h_bank = [h_first, h_second]
+        for h in range(2):
+            for t in range(PACK):
+                copy = nc.vector.tensor_copy if (t, h) in C_DVE else nc.scalar.copy
+                copy(hw[t][:, halves[h]], h_bank[h][t][:])
+
+        out_rows = out_0.rearrange("(p t) c -> p t c", t=PACK)
+        out_codes = sb.tile([P, S], U32, name="out_codes", align_bytes=64)
+        out_plane = sb.tile([P, S], U8, name="out_plane", align_bytes=64)
+        out_words = words_of(out_1)
+        chunks = range(len(PIECES))
+        pp = [sb.tile([P, PACK, PIECES[c][1]], F32, name=f"pp{c}", tag=f"pp{c}") for c in chunks]
+        prod = [sb.tile([P, PACK, HALF], F32, name=f"prod{h}") for h in range(2)]
+        den = [sb.tile([P, PACK, PIECES[c][1]], F32, name=f"den{c}") for c in chunks]
+        root = [sb.tile([P, PACK, PIECES[c][1]], F32, name=f"root{c}", tag=f"root{c}", align_bytes=64) for c in chunks]
+        inv = [sb.tile([P, PACK, PIECES[c][1]], F32, name=f"inv{c}") for c in chunks]
+        pa = []
+        res = {}
+
+        def columns(c):
+            return slice(PIECES[c][0], PIECES[c][0] + PIECES[c][1])
+
+        def inner(c):
+            return slice(PIECES[c][0] % HALF, PIECES[c][0] % HALF + PIECES[c][1])
+
+        def square_h(h):
+            for t in range(PACK):
+                if (t, h) in HH_DVE:
+                    nc.vector.tensor_tensor(hh[h][:, t, :], hw[t][:, halves[h]], h_bank[h][t][:], ALU.mult)
+                else:
+                    nc.scalar.activation(out=hh[h][:, t, :], in_=h_bank[h][t][:], func=ACT.Square)
+
+        def fetch_pa(h):
+            pa.append(sb.tile([P, PACK, HALF], F32, name=f"pa{h}", tag="pp0" if h else "pa0"))
+            for t in range(PACK):
+                fetch((t, h) in B_ACT, pa[h][:, t, :], hw[t], entries(l_n3, h * HALF, HALF))
+
+        def denominator(c):
+            h = PIECES[c][0] // HALF
+            nc.scalar.activation(out=pp[c][:], in_=pa[h][:, :, inner(c)], func=ACT.Square)
+            nc.vector.tensor_tensor(den[c][:], pp[c][:], hh[h][:, :, inner(c)], ALU.add)
+
+        def numerator(h):
+            for t in range(PACK):
+                nc.vector.tensor_tensor(prod[h][:, t, :], pa[h][:, t, :], h_bank[h][t][:], ALU.mult)
+
+        def inverse_root(c):
+            nc.scalar.activation(out=root[c][:], in_=den[c][:], func=ACT.Abs_reciprocal_sqrt, scale=0.5, bias=0.25)
+
+        def invert(c):
+            nc.scalar.activation(out=inv[c][:], in_=root[c][:], func=ACT.Square)
+
+        def finish(c):
+            res[c] = sb.tile([P, PACK, PIECES[c][1]], F32, name=f"res{c}", tag=f"pp{c + 2}" if c < 2 else f"res{c}")
+            nc.vector.tensor_tensor(res[c][:], prod[PIECES[c][0] // HALF][:, :, inner(c)], inv[c][:], ALU.mult)
+            nc.sync.dma_start(out_rows[:, :, columns(c)], res[c][:])
+
+        def planes(c):
+            grouped = sb.tile([P, PACK * PIECES[c][1]], BF16, name=f"grouped{c}", tag="root3" if c == 1 else f"grouped{c}", align_bytes=64)
+            interleave(nc.scalar.copy if c in IL_ACT else nc.vector.tensor_copy, grouped, res[c][:])
+            nc.vector.quantize_mx(out=out_codes[:, columns(c)].bitcast(FP8X4), scales=out_plane[:, columns(c)], in_=grouped[:])
+            if columns(c).stop % HALF == 0:
+                half = halves[PIECES[c][0] // HALF]
+                nc.sync.dma_start(out_words[:, half], out_codes[:, half].bitcast(I32))
+
+        square_h(0)
+        fetch_pa(0)
+        denominator(0)
+        denominator(1)
+        numerator(0)
+        square_h(1)
+        fetch_pa(1)
+        inverse_root(0)
+        inverse_root(1)
+        invert(0)
+        denominator(2)
+        denominator(3)
+        invert(1)
+        inverse_root(2)
+        inverse_root(3)
+        invert(2)
+        invert(3)
+        numerator(1)
+        finish(0)
+        finish(1)
+        finish(2)
+        finish(3)
+        planes(0)
+        planes(1)
+        planes(2)
+        planes(3)
+        for q in range(4):
+            queue = nc.scalar if q % 2 else nc.sync
+            queue.dma_start(out_2[0, 4 * q : 4 * q + 4, :].bitcast(I32), out_plane[32 * q : 32 * q + 4, :].bitcast(I32))

@@ -57,6 +57,8 @@ def tile_picked_hashhopdharm_none_po_kernel(
         x_plane = sb.tile([P, S], U8, name="x_plane", align_bytes=64)
         for tile in (table_bytes, w_raw_bytes, x_plane):
             nc.vector.memset(tile[:].bitcast(I32), 0)
+        warm = sb.tile([P, 2], F32, name="warm")
+        nc.vector.memset(warm[:, 0:1], 0.0)
 
         x_rows = x_scales[0].rearrange("(m e) c -> e m c", e=2)
         for e in range(2):
@@ -72,6 +74,7 @@ def tile_picked_hashhopdharm_none_po_kernel(
                 queues[q // 2].dma_start(w_raw_bytes[32 * q : 32 * q + 4, :].bitcast(I32), dram[0, 4 * q : 4 * q + 4, :].bitcast(I32))
 
         load_plane((nc.scalar, nc.gpsimd), w1_scales)
+        nc.scalar.activation(out=warm[:, 1:2], in_=warm[:, 0:1], func=ACT.Sigmoid)
         gain = sb.tile([P, PACK], F32, name="gain")
         nc.gpsimd.dma_start(gain[:], gn.rearrange("(p t) o -> p (t o)", t=PACK))
 
@@ -132,6 +135,7 @@ def tile_picked_hashhopdharm_none_po_kernel(
         w2_plane = sb.tile([P, N], U8, name="w2_plane", tag="y_n1_1", align_bytes=64)
         w2_codes = sb.tile([P, N], U32, name="w2_codes", tag="st3", align_bytes=64)
         deal(nc.scalar.copy, w2_codes, w2_raw_words)
+        nc.scalar.activation(out=warm[:, 1:2], in_=sig[3][1][:, 0:1], func=ACT.Abs_reciprocal_sqrt)
         deal(nc.vector.tensor_copy, w2_plane, w_raw_bytes)
 
         def interleave(copy, grouped, planes):

@@ -24,6 +24,7 @@ B_ACT = ((2, 0), (3, 0), (3, 1))
 HH_DVE = ((0, 0), (1, 0))
 C_DVE = ((0, 1), (1, 1))
 Y_DVE = ((0, 0), (1, 0))
+SUB_POOL = ()
 IL_ACT = (1, 2)
 PIECES = ((0, 128), (128, 128), (256, 128), (384, 128))
 
@@ -49,32 +50,33 @@ def tile_picked_hashhopdharm_none_po_kernel(
         l_n1 = lists.tile([P, S // 16], U16, name="l_n1")
         l_n2 = lists.tile([P, S // 16], U16, name="l_n2")
         l_n3 = lists.tile([P, S // 16], U16, name="l_n3")
-        for tile, dram in ((l_offs, offs), (l_n1, n1), (l_n2, n2), (l_n3, n3)):
+        table_words = early.tile([P, T], U32, name="table_words", align_bytes=64, offset=4096)
+        nc.sync.dma_start(l_offs[:], offs)
+        nc.sync.dma_start(table_words[:].bitcast(I32), words_of(x_words))
+        for tile, dram in ((l_n1, n1), (l_n2, n2), (l_n3, n3)):
             nc.sync.dma_start(tile[:], dram)
+        w1_raw_words = sb.tile([P, H], U32, name="w1_raw_words", align_bytes=64)
+        nc.sync.dma_start(w1_raw_words[:].bitcast(I32), words_of(w1_words))
 
-        table_bytes = sb.tile([P, T], U8, name="table_bytes", tag="x_side", align_bytes=64)
+        table_bytes = early.tile([P, T], U8, name="table_bytes", align_bytes=64, offset=1024)
         w_raw_bytes = sb.tile([P, H], U8, name="w_raw_bytes", align_bytes=64)
         x_plane = sb.tile([P, S], U8, name="x_plane", align_bytes=64)
-        for tile in (table_bytes, w_raw_bytes, x_plane):
-            nc.vector.memset(tile[:].bitcast(I32), 0)
         warm = sb.tile([P, 2], F32, name="warm")
+        nc.vector.memset(table_bytes[:].bitcast(I32), 0)
         nc.vector.memset(warm[:, 0:1], 0.0)
+        nc.vector.memset(w_raw_bytes[:].bitcast(I32), 0)
+        nc.vector.memset(x_plane[:].bitcast(I32), 0)
 
         x_rows = x_scales[0].rearrange("(m e) c -> e m c", e=2)
         for e in range(2):
             nc.scalar.dma_start(table_bytes[e:P:16, :].bitcast(I32), x_rows[e].bitcast(I32))
-
-        table_words = early.tile([P, T], U32, name="table_words", align_bytes=64, offset=0)
-        nc.sync.dma_start(table_words[:].bitcast(I32), words_of(x_words))
-        w1_raw_words = sb.tile([P, H], U32, name="w1_raw_words", align_bytes=64)
-        nc.sync.dma_start(w1_raw_words[:].bitcast(I32), words_of(w1_words))
-
-        def load_plane(queues, dram):
-            for q in range(4):
-                queues[q // 2].dma_start(w_raw_bytes[32 * q : 32 * q + 4, :].bitcast(I32), dram[0, 4 * q : 4 * q + 4, :].bitcast(I32))
-
-        load_plane((nc.scalar, nc.gpsimd), w1_scales)
         nc.scalar.activation(out=warm[:, 1:2], in_=warm[:, 0:1], func=ACT.Sigmoid)
+
+        def load_plane(queue, dram):
+            for q in range(4):
+                queue.dma_start(w_raw_bytes[32 * q : 32 * q + 4, :].bitcast(I32), dram[0, 4 * q : 4 * q + 4, :].bitcast(I32))
+
+        load_plane(nc.scalar, w1_scales)
         gain = sb.tile([P, PACK], F32, name="gain")
         nc.gpsimd.dma_start(gain[:], gn.rearrange("(p t) o -> p (t o)", t=PACK))
 
@@ -85,20 +87,20 @@ def tile_picked_hashhopdharm_none_po_kernel(
         for q in range(4):
             rows = slice(32 * q, 32 * q + 2)
             nc.vector.tensor_copy(x_plane[rows, :].bitcast(I32), picked_bytes[rows, :].bitcast(I32))
+        w2_raw_words = early.tile([P, N], U32, name="w2_raw_words", align_bytes=64, offset=2048)
+        nc.sync.dma_start(w2_raw_words[:].bitcast(I32), words_of(w2_words))
 
-        def deal(copy, dealt, raw):
-            copy(dealt[:].rearrange("p (t m) -> p m t", t=PACK), raw[:].rearrange("p (m t) -> p m t", t=PACK))
+        def deal(dealt, raw):
+            nc.scalar.copy(dealt[:].rearrange("p (t m) -> p m t", t=PACK), raw[:].rearrange("p (m t) -> p m t", t=PACK))
 
-        w1_plane = [early.tile([P, P], U8, name=f"w1_plane{t}", align_bytes=64, offset=P * t) for t in range(PACK)]
+        w1_plane = [early.tile([P, P], U8, name=f"w1_plane{t}", align_bytes=64, offset=4096 + P * t) for t in range(PACK)]
         w1_codes = sb.tile([P, H], U32, name="w1_codes", align_bytes=64)
-        deal(nc.scalar.copy, w1_codes, w1_raw_words)
-        x_codes = sb.tile([P, S], U32, name="x_codes", tag="x_side", align_bytes=64)
+        deal(w1_codes, w1_raw_words)
+        x_codes = early.tile([P, S], U32, name="x_codes", align_bytes=64, offset=0)
         nc.vector.tensor_copy(x_codes[:], table_words[:].indirect(l_offs[:]))
         for t in range(PACK):
             nc.vector.tensor_copy(w1_plane[t][:], w_raw_bytes[:, t:H:PACK])
-        w2_raw_words = early.tile([P, N], U32, name="w2_raw_words", align_bytes=64, offset=H)
-        nc.sync.dma_start(w2_raw_words[:].bitcast(I32), words_of(w2_words))
-        load_plane((nc.sync, nc.sync), w2_scales)
+        load_plane(nc.sync, w2_scales)
 
         halves = [slice(h * HALF, (h + 1) * HALF) for h in range(2)]
         y_bank = [[ps.tile([P, HALF], F32, name=f"y_bank{t}_{h}", tag=f"bank{t}_{h}") for h in range(2)] for t in range(PACK)]
@@ -128,15 +130,18 @@ def tile_picked_hashhopdharm_none_po_kernel(
             for h in range(2):
                 fetch((t, h) in A_ACT, y_n1[t][:, halves[h]], y[t], entries(l_n1, h * HALF, HALF))
             for h in range(2):
-                nc.vector.tensor_tensor(st[t][:, halves[h]], y_n1[t][:, halves[h]], y_bank[t][h][:], ALU.subtract)
+                if (t, h) in SUB_POOL:
+                    nc.gpsimd.tensor_tensor(st[t][:, halves[h]], y_n1[t][:, halves[h]], y[t][:, halves[h]], ALU.subtract)
+                else:
+                    nc.vector.tensor_tensor(st[t][:, halves[h]], y_n1[t][:, halves[h]], y_bank[t][h][:], ALU.subtract)
         for t in range(PACK):
             for h in range(2):
                 nc.scalar.activation(out=sig[t][h][:], in_=st[t][:].indirect(entries(l_n2, h * HALF, HALF)), func=ACT.Sigmoid)
         w2_plane = sb.tile([P, N], U8, name="w2_plane", tag="y_n1_1", align_bytes=64)
         w2_codes = sb.tile([P, N], U32, name="w2_codes", tag="st3", align_bytes=64)
-        deal(nc.scalar.copy, w2_codes, w2_raw_words)
+        deal(w2_codes, w2_raw_words)
         nc.scalar.activation(out=warm[:, 1:2], in_=sig[3][1][:, 0:1], func=ACT.Abs_reciprocal_sqrt)
-        deal(nc.vector.tensor_copy, w2_plane, w_raw_bytes)
+        nc.vector.tensor_copy(w2_plane[:].rearrange("p (t m) -> p t m", t=PACK), w_raw_bytes[:].rearrange("p (m t) -> p t m", t=PACK))
 
         def interleave(copy, grouped, planes):
             copy(grouped[:].rearrange("p (c i t) -> p c t i", i=4, t=PACK), planes.rearrange("p t (c i) -> p c t i", i=4))
@@ -237,7 +242,7 @@ def tile_picked_hashhopdharm_none_po_kernel(
             nc.vector.quantize_mx(out=out_codes[:, columns(c)].bitcast(FP8X4), scales=out_plane[:, columns(c)], in_=grouped[:])
             if columns(c).stop % HALF == 0:
                 half = halves[PIECES[c][0] // HALF]
-                nc.sync.dma_start(out_words[:, half], out_codes[:, half].bitcast(I32))
+                nc.scalar.dma_start(out_words[:, half], out_codes[:, half].bitcast(I32))
 
         square_h(0)
         fetch_pa(0)

@@ -46,63 +46,68 @@ def tile_picked_hashhopdharm_none_po_kernel(
         def words_of(dram):
             return dram[0].rearrange("p c r -> p (c r)").bitcast(I32)
 
+        halves = [slice(h * HALF, (h + 1) * HALF) for h in range(2)]
         l_offs = lists.tile([P, S // 16], U16, name="l_offs")
         l_n1 = lists.tile([P, S // 16], U16, name="l_n1")
         l_n2 = lists.tile([P, S // 16], U16, name="l_n2")
         l_n3 = lists.tile([P, S // 16], U16, name="l_n3")
-        table_words = early.tile([P, T], U32, name="table_words", align_bytes=64, offset=4096)
-        nc.sync.dma_start(l_offs[:], offs)
-        nc.sync.dma_start(table_words[:].bitcast(I32), words_of(x_words))
-        for tile, dram in ((l_n1, n1), (l_n2, n2), (l_n3, n3)):
-            nc.sync.dma_start(tile[:], dram)
-        w1_raw_words = sb.tile([P, H], U32, name="w1_raw_words", align_bytes=64)
-        nc.sync.dma_start(w1_raw_words[:].bitcast(I32), words_of(w1_words))
-
         table_bytes = early.tile([P, T], U8, name="table_bytes", align_bytes=64, offset=1024)
-        w_raw_bytes = sb.tile([P, H], U8, name="w_raw_bytes", align_bytes=64)
+        table_words = early.tile([P, T], U32, name="table_words", align_bytes=64, offset=4608)
+        w1_raw_words = sb.tile([P, H], U32, name="w1_raw_words", align_bytes=64)
+        w1_raw_bytes = early.tile([P, H], U8, name="w1_raw_bytes", align_bytes=64, offset=3072)
+        nc.sync.dma_start(l_offs[:], offs)
+        nc.sync.dma_start(table_bytes[:].bitcast(I32), x_scales[0].bitcast(I32).unsqueeze(1).to_broadcast([16, 8, T // 4]))
+        nc.sync.dma_start(l_n1[:], n1)
+        nc.sync.dma_start(table_words[:].bitcast(I32), words_of(x_words))
+        nc.sync.dma_start(w1_raw_words[:].bitcast(I32), words_of(w1_words))
+        nc.sync.dma_start(l_n2[:], n2)
+        nc.sync.dma_start(l_n3[:], n3)
+
+        def load_scale_rows(queue, raw, dram):
+            for q in range(4):
+                rows = dram[0, 4 * q : 4 * q + 4, :].bitcast(I32)
+                queue.dma_start(raw[32 * q : 32 * q + 32, :].bitcast(I32), rows.unsqueeze(0).to_broadcast([8, 4, H // 4]))
+
+        load_scale_rows(nc.scalar, w1_raw_bytes, w1_scales)
+
         x_plane = sb.tile([P, S], U8, name="x_plane", align_bytes=64)
         warm = sb.tile([P, 2], F32, name="warm")
-        nc.vector.memset(table_bytes[:].bitcast(I32), 0)
         nc.vector.memset(warm[:, 0:1], 0.0)
-        nc.vector.memset(w_raw_bytes[:].bitcast(I32), 0)
         nc.vector.memset(x_plane[:].bitcast(I32), 0)
-
-        x_rows = x_scales[0].rearrange("(m e) c -> e m c", e=2)
-        for e in range(2):
-            nc.scalar.dma_start(table_bytes[e:P:16, :].bitcast(I32), x_rows[e].bitcast(I32))
         nc.scalar.activation(out=warm[:, 1:2], in_=warm[:, 0:1], func=ACT.Sigmoid)
-
-        def load_plane(queue, dram):
-            for q in range(4):
-                queue.dma_start(w_raw_bytes[32 * q : 32 * q + 4, :].bitcast(I32), dram[0, 4 * q : 4 * q + 4, :].bitcast(I32))
-
-        load_plane(nc.scalar, w1_scales)
         gain = sb.tile([P, PACK], F32, name="gain")
         nc.gpsimd.dma_start(gain[:], gn.rearrange("(p t) o -> p (t o)", t=PACK))
 
         picked_bytes = sb.tile([P, S], U8, name="picked_bytes", align_bytes=64)
         nc.vector.tensor_copy(picked_bytes[:], table_bytes[:].indirect(l_offs[:]))
-        for e in range(2):
-            nc.sync.dma_start(x_plane[2 + e : P : 32, :].bitcast(I32), picked_bytes[16 + e : P : 32, :].bitcast(I32))
+        for r in range(1, 4):
+            nc.scalar.dma_start(x_plane[r:P:32, :].bitcast(I32), picked_bytes[8 * r : P : 32, :].bitcast(I32))
         for q in range(4):
-            rows = slice(32 * q, 32 * q + 2)
+            rows = slice(32 * q, 32 * q + 1)
             nc.vector.tensor_copy(x_plane[rows, :].bitcast(I32), picked_bytes[rows, :].bitcast(I32))
-        w2_raw_words = early.tile([P, N], U32, name="w2_raw_words", align_bytes=64, offset=2048)
+
+        def deal_words(dealt, raw, first, count):
+            nc.scalar.copy(
+                dealt[:].rearrange("p (t m) -> p m t", t=count),
+                raw[:].rearrange("p (m t) -> p m t", t=PACK)[:, :, first : first + count],
+            )
+
+        def deal_bytes(dealt, raw):
+            nc.vector.tensor_copy(dealt[:].rearrange("p (t m) -> p t m", t=PACK), raw[:].rearrange("p (m t) -> p t m", t=PACK))
+
+        w1_plane = sb.tile([P, H], U8, name="w1_plane", align_bytes=64)
+        deal_bytes(w1_plane, w1_raw_bytes)
+        w1_codes = [sb.tile([P, 2 * P], U32, name=f"w1_codes{u}", align_bytes=64) for u in range(2)]
+        for u in range(2):
+            deal_words(w1_codes[u], w1_raw_words, 2 * u, 2)
+        x_codes = [early.tile([P, HALF], U32, name=f"x_codes{h}", align_bytes=64, offset=2304 + 1024 * h) for h in range(2)]
+        for h in range(2):
+            nc.vector.tensor_copy(x_codes[h][:], table_words[:].indirect(entries(l_offs, h * HALF, HALF)))
+        w2_raw_words = early.tile([P, N], U32, name="w2_raw_words", align_bytes=64, offset=4608)
+        w2_raw_bytes = early.tile([P, N], U8, name="w2_raw_bytes", align_bytes=64, offset=6656)
         nc.sync.dma_start(w2_raw_words[:].bitcast(I32), words_of(w2_words))
+        load_scale_rows(nc.sync, w2_raw_bytes, w2_scales)
 
-        def deal(dealt, raw):
-            nc.scalar.copy(dealt[:].rearrange("p (t m) -> p m t", t=PACK), raw[:].rearrange("p (m t) -> p m t", t=PACK))
-
-        w1_plane = [early.tile([P, P], U8, name=f"w1_plane{t}", align_bytes=64, offset=4096 + P * t) for t in range(PACK)]
-        w1_codes = sb.tile([P, H], U32, name="w1_codes", align_bytes=64)
-        deal(w1_codes, w1_raw_words)
-        x_codes = early.tile([P, S], U32, name="x_codes", align_bytes=64, offset=0)
-        nc.vector.tensor_copy(x_codes[:], table_words[:].indirect(l_offs[:]))
-        for t in range(PACK):
-            nc.vector.tensor_copy(w1_plane[t][:], w_raw_bytes[:, t:H:PACK])
-        load_plane(nc.sync, w2_scales)
-
-        halves = [slice(h * HALF, (h + 1) * HALF) for h in range(2)]
         y_bank = [[ps.tile([P, HALF], F32, name=f"y_bank{t}_{h}", tag=f"bank{t}_{h}") for h in range(2)] for t in range(PACK)]
         y = [sb.tile([P, S], F32, name=f"y{t}") for t in range(PACK)]
         y_n1 = [sb.tile([P, S], F32, name=f"y_n1_{t}", tag=f"y_n1_{t}", align_bytes=64) for t in range(PACK)]
@@ -112,8 +117,9 @@ def tile_picked_hashhopdharm_none_po_kernel(
         for t in range(PACK):
             for h in range(2):
                 nc.tensor.matmul_mx(
-                    out=y_bank[t][h][:], lhsT=w1_codes[:, P * t : P * (t + 1)].bitcast(FP8X4), lhsT_scale=w1_plane[t][:],
-                    rhs=x_codes[:, halves[h]].bitcast(FP8X4), rhs_scale=x_plane[:, halves[h]], start=True, stop=True,
+                    out=y_bank[t][h][:], lhsT=w1_codes[t // 2][:, P * (t % 2) : P * (t % 2 + 1)].bitcast(FP8X4),
+                    lhsT_scale=w1_plane[:, P * t : P * (t + 1)],
+                    rhs=x_codes[h][:].bitcast(FP8X4), rhs_scale=x_plane[:, halves[h]], start=True, stop=True,
                 )
 
         def fetch(on_scalar, out, window, offsets):
@@ -139,9 +145,9 @@ def tile_picked_hashhopdharm_none_po_kernel(
                 nc.scalar.activation(out=sig[t][h][:], in_=st[t][:].indirect(entries(l_n2, h * HALF, HALF)), func=ACT.Sigmoid)
         w2_plane = sb.tile([P, N], U8, name="w2_plane", tag="y_n1_1", align_bytes=64)
         w2_codes = sb.tile([P, N], U32, name="w2_codes", tag="st3", align_bytes=64)
-        deal(w2_codes, w2_raw_words)
+        deal_words(w2_codes, w2_raw_words, 0, PACK)
         nc.scalar.activation(out=warm[:, 1:2], in_=sig[3][1][:, 0:1], func=ACT.Abs_reciprocal_sqrt)
-        nc.vector.tensor_copy(w2_plane[:].rearrange("p (t m) -> p t m", t=PACK), w_raw_bytes[:].rearrange("p (m t) -> p t m", t=PACK))
+        deal_bytes(w2_plane, w2_raw_bytes)
 
         def interleave(copy, grouped, planes):
             copy(grouped[:].rearrange("p (c i t) -> p c t i", i=4, t=PACK), planes.rearrange("p t (c i) -> p c t i", i=4))

@@ -20,11 +20,13 @@ PACK = 4
 HALF = S // 2
 CHUNK = S // 4
 A_ACT = ((2, 0), (2, 1))
-B_ACT = ((2, 0), (3, 0), (3, 1))
+B_ACT = ((1, 0), (3, 0), (3, 1))
 HH_DVE = ((0, 0), (1, 0))
-C_DVE = ((0, 1), (1, 1))
+C_DVE = ((0, 1), (2, 1))
 Y_DVE = ((0, 0), (1, 0))
 SUB_POOL = ()
+HH_POOL = ((2, 1), (3, 1))
+HH_TAG = ("hh0", "hh1")
 IL_ACT = (1, 2)
 PIECES = ((0, 128), (128, 128), (256, 128), (384, 128))
 
@@ -143,11 +145,11 @@ def tile_picked_hashhopdharm_none_po_kernel(
         for t in range(PACK):
             for h in range(2):
                 nc.scalar.activation(out=sig[t][h][:], in_=st[t][:].indirect(entries(l_n2, h * HALF, HALF)), func=ACT.Sigmoid)
-        w2_plane = sb.tile([P, N], U8, name="w2_plane", tag="y_n1_1", align_bytes=64)
-        w2_codes = sb.tile([P, N], U32, name="w2_codes", tag="st3", align_bytes=64)
-        deal_words(w2_codes, w2_raw_words, 0, PACK)
+        w2_plane = sb.tile([P, N], U8, name="w2_plane", align_bytes=64)
+        w2_codes = sb.tile([P, N], U32, name="w2_codes", align_bytes=64)
+        for dealt, raw in ((w2_codes, w2_raw_words), (w2_plane, w2_raw_bytes)):
+            nc.gpsimd.tensor_copy(dealt[:].rearrange("p (t m) -> p t m", t=PACK), raw[:].rearrange("p (m t) -> p t m", t=PACK))
         nc.scalar.activation(out=warm[:, 1:2], in_=sig[3][1][:, 0:1], func=ACT.Abs_reciprocal_sqrt)
-        deal_bytes(w2_plane, w2_raw_bytes)
 
         def interleave(copy, grouped, planes):
             copy(grouped[:].rearrange("p (c i t) -> p c t i", i=4, t=PACK), planes.rearrange("p t (c i) -> p c t i", i=4))
@@ -160,31 +162,34 @@ def tile_picked_hashhopdharm_none_po_kernel(
                 )
 
         def group_z(h, start, width):
-            grouped = sb.tile([P, PACK * width], BF16, name=f"z_grouped{h}_{start}", align_bytes=64)
+            grouped = sb.tile([P, PACK * width], BF16, name=f"z_grouped{h}_{start}", tag=f"z_grouped{h}_{start}", align_bytes=64)
             interleave(nc.vector.tensor_copy, grouped, z[h][:, :, start : start + width])
             return grouped
 
-        def second_product(banks, grouped, h, start, width):
+        def quantise_z(grouped, h, start, width):
             codes = sb.tile([P, width], U32, name=f"z_codes{h}_{start}", align_bytes=64)
             plane = sb.tile([P, width], U8, name=f"z_plane{h}_{start}", align_bytes=64)
             nc.vector.quantize_mx(out=codes[:].bitcast(FP8X4), scales=plane[:], in_=grouped[:])
+            return codes, plane, slice(start, start + width)
+
+        def second_product(banks, pieces):
             for t in range(PACK):
                 cols = slice(P * t, P * (t + 1))
-                nc.tensor.matmul_mx(
-                    out=banks[t][:, start : start + width], lhsT=w2_codes[:, cols].bitcast(FP8X4), lhsT_scale=w2_plane[:, cols],
-                    rhs=codes[:].bitcast(FP8X4), rhs_scale=plane[:], start=True, stop=True,
-                )
+                for codes, plane, where in pieces:
+                    nc.tensor.matmul_mx(
+                        out=banks[t][:, where], lhsT=w2_codes[:, cols].bitcast(FP8X4), lhsT_scale=w2_plane[:, cols],
+                        rhs=codes[:].bitcast(FP8X4), rhs_scale=plane[:], start=True, stop=True,
+                    )
 
         hw = [sb.tile([P, S], F32, name=f"h{t}") for t in range(PACK)]
-        hh = [sb.tile([P, PACK, HALF], F32, name=f"hh{h}") for h in range(2)]
+        hh = []
         h_first = [ps.tile([P, HALF], F32, name=f"h_first{t}", tag=f"bank{t}_0") for t in range(PACK)]
         make_z(0)
-        second_product(h_first, group_z(0, 0, HALF), 0, 0, HALF)
+        second_product(h_first, [quantise_z(group_z(0, 0, HALF), 0, 0, HALF)])
         make_z(1)
         h_second = [ps.tile([P, HALF], F32, name=f"h_second{t}", tag=f"bank{t}_1") for t in range(PACK)]
         z_last = [group_z(1, start, CHUNK) for start in (0, CHUNK)]
-        second_product(h_second, z_last[0], 1, 0, CHUNK)
-        second_product(h_second, z_last[1], 1, CHUNK, CHUNK)
+        second_product(h_second, [quantise_z(z_last[i], 1, i * CHUNK, CHUNK) for i in range(2)])
         h_bank = [h_first, h_second]
         for h in range(2):
             for t in range(PACK):
@@ -211,8 +216,11 @@ def tile_picked_hashhopdharm_none_po_kernel(
             return slice(PIECES[c][0] % HALF, PIECES[c][0] % HALF + PIECES[c][1])
 
         def square_h(h):
+            hh.append(sb.tile([P, PACK, HALF], F32, name=f"hh{h}", tag=HH_TAG[h], align_bytes=64))
             for t in range(PACK):
-                if (t, h) in HH_DVE:
+                if (t, h) in HH_POOL:
+                    nc.gpsimd.tensor_tensor(hh[h][:, t, :], hw[t][:, halves[h]], hw[t][:, halves[h]], ALU.mult)
+                elif (t, h) in HH_DVE:
                     nc.vector.tensor_tensor(hh[h][:, t, :], hw[t][:, halves[h]], h_bank[h][t][:], ALU.mult)
                 else:
                     nc.scalar.activation(out=hh[h][:, t, :], in_=h_bank[h][t][:], func=ACT.Square)

from contextlib import ExitStack

import concourse.mybir as mybir

K, T, S, N, H = 512, 2048, 512, 512, 512
FLOPS = 2 * K * H * S + 2 * H * N * S

F32 = mybir.dt.float32
BF16 = mybir.dt.bfloat16
I32 = mybir.dt.int32
U32 = mybir.dt.uint32
U16 = mybir.dt.uint16
U8 = mybir.dt.uint8
FP8X4 = mybir.dt.float8_e4m3fn_x4
ACT = mybir.ActivationFunctionType
ALU = mybir.AluOpType

P = 128
PACK = 4
HALF = S // 2
CHUNK = S // 4
A_ACT = ((2, 0), (2, 1))
B_ACT = ((1, 0), (3, 0), (3, 1))
HH_DVE = ((0, 0), (1, 0))
C_DVE = ((0, 1), (2, 1))
Y_DVE = ((0, 0), (1, 0))
SUB_POOL = ()
HH_POOL = ((2, 1), (3, 1))
HH_TAG = ("hh0", "hh1")
IL_ACT = (1, 2)
PIECES = ((0, 128), (128, 128), (256, 128), (384, 128))


def entries(lst, start, count):
    return lst[:, start // 16 : (start + count) // 16]


def tile_picked_hashhopdharm_none_po_kernel(
    tc, x_words, x_scales, w1_words, w1_scales, gn, w2_words, w2_scales, offs, n1, n2, n3, out_0, out_1, out_2
):
    nc = tc.nc
    with ExitStack() as ctx:
        lists = ctx.enter_context(tc.tile_pool(name="lists", bufs=1))
        sb = ctx.enter_context(tc.tile_pool(name="sb", bufs=1))
        early = ctx.enter_context(tc.tile_pool(name="early", bufs=1))
        ps = ctx.enter_context(tc.psum_pool(name="ps", bufs=1))

        def words_of(dram):
            return dram[0].rearrange("p c r -> p (c r)").bitcast(I32)

        halves = [slice(h * HALF, (h + 1) * HALF) for h in range(2)]
        l_offs = lists.tile([P, S // 16], U16, name="l_offs")
        l_n1 = lists.tile([P, S // 16], U16, name="l_n1")
        l_n2 = lists.tile([P, S // 16], U16, name="l_n2")
        l_n3 = lists.tile([P, S // 16], U16, name="l_n3")
        table_bytes = early.tile([P, T], U8, name="table_bytes", align_bytes=64, offset=1024)
        table_words = early.tile([P, T], U32, name="table_words", align_bytes=64, offset=4608)
        w1_raw_words = sb.tile([P, H], U32, name="w1_raw_words", align_bytes=64)
        w1_raw_bytes = early.tile([P, H], U8, name="w1_raw_bytes", align_bytes=64, offset=3072)
        nc.sync.dma_start(l_offs[:], offs)
        nc.sync.dma_start(table_bytes[:].bitcast(I32), x_scales[0].bitcast(I32).unsqueeze(1).to_broadcast([16, 8, T // 4]))
        nc.sync.dma_start(l_n1[:], n1)
        nc.sync.dma_start(table_words[:].bitcast(I32), words_of(x_words))
        nc.sync.dma_start(w1_raw_words[:].bitcast(I32), words_of(w1_words))
        nc.sync.dma_start(l_n2[:], n2)
        nc.sync.dma_start(l_n3[:], n3)

        def load_scale_rows(queue, raw, dram):
            for q in range(4):
                rows = dram[0, 4 * q : 4 * q + 4, :].bitcast(I32)
                queue.dma_start(raw[32 * q : 32 * q + 32, :].bitcast(I32), rows.unsqueeze(0).to_broadcast([8, 4, H // 4]))

        load_scale_rows(nc.scalar, w1_raw_bytes, w1_scales)

        x_plane = sb.tile([P, S], U8, name="x_plane", align_bytes=64)
        warm = sb.tile([P, 2], F32, name="warm")
        nc.vector.memset(warm[:, 0:1], 0.0)
        nc.vector.memset(x_plane[:].bitcast(I32), 0)
        nc.scalar.activation(out=warm[:, 1:2], in_=warm[:, 0:1], func=ACT.Sigmoid)
        gain = sb.tile([P, PACK], F32, name="gain")
        nc.gpsimd.dma_start(gain[:], gn.rearrange("(p t) o -> p (t o)", t=PACK))

        picked_bytes = sb.tile([P, S], U8, name="picked_bytes", align_bytes=64)
        nc.vector.tensor_copy(picked_bytes[:], table_bytes[:].indirect(l_offs[:]))
        for r in range(1, 4):
            nc.scalar.dma_start(x_plane[r:P:32, :].bitcast(I32), picked_bytes[8 * r : P : 32, :].bitcast(I32))
        for q in range(4):
            rows = slice(32 * q, 32 * q + 1)
            nc.vector.tensor_copy(x_plane[rows, :].bitcast(I32), picked_bytes[rows, :].bitcast(I32))

        def deal_words(dealt, raw, first, count):
            nc.scalar.copy(
                dealt[:].rearrange("p (t m) -> p m t", t=count),
                raw[:].rearrange("p (m t) -> p m t", t=PACK)[:, :, first : first + count],
            )

        def deal_bytes(dealt, raw):
            nc.vector.tensor_copy(dealt[:].rearrange("p (t m) -> p t m", t=PACK), raw[:].rearrange("p (m t) -> p t m", t=PACK))

        w1_plane = sb.tile([P, H], U8, name="w1_plane", align_bytes=64)
        deal_bytes(w1_plane, w1_raw_bytes)
        w1_codes = [sb.tile([P, 2 * P], U32, name=f"w1_codes{u}", align_bytes=64) for u in range(2)]
        for u in range(2):
            deal_words(w1_codes[u], w1_raw_words, 2 * u, 2)
        x_codes = [early.tile([P, HALF], U32, name=f"x_codes{h}", align_bytes=64, offset=2304 + 1024 * h) for h in range(2)]
        for h in range(2):
            nc.vector.tensor_copy(x_codes[h][:], table_words[:].indirect(entries(l_offs, h * HALF, HALF)))
        w2_raw_words = early.tile([P, N], U32, name="w2_raw_words", align_bytes=64, offset=4608)
        w2_raw_bytes = early.tile([P, N], U8, name="w2_raw_bytes", align_bytes=64, offset=6656)
        nc.sync.dma_start(w2_raw_words[:].bitcast(I32), words_of(w2_words))
        load_scale_rows(nc.sync, w2_raw_bytes, w2_scales)

        y_bank = [[ps.tile([P, HALF], F32, name=f"y_bank{t}_{h}", tag=f"bank{t}_{h}") for h in range(2)] for t in range(PACK)]
        y = [sb.tile([P, S], F32, name=f"y{t}") for t in range(PACK)]
        y_n1 = [sb.tile([P, S], F32, name=f"y_n1_{t}", tag=f"y_n1_{t}", align_bytes=64) for t in range(PACK)]
        st = [sb.tile([P, S], F32, name=f"st{t}", tag=f"st{t}", align_bytes=64) for t in range(PACK)]
        sig = [[sb.tile([P, HALF], F32, name=f"sig{t}_{h}") for h in range(2)] for t in range(PACK)]
        z = [sb.tile([P, PACK, HALF], BF16, name=f"z{h}") for h in range(2)]
        for t in range(PACK):
            for h in range(2):
                nc.tensor.matmul_mx(
                    out=y_bank[t][h][:], lhsT=w1_codes[t // 2][:, P * (t % 2) : P * (t % 2 + 1)].bitcast(FP8X4),
                    lhsT_scale=w1_plane[:, P * t : P * (t + 1)],
                    rhs=x_codes[h][:].bitcast(FP8X4), rhs_scale=x_plane[:, halves[h]], start=True, stop=True,
                )

        def fetch(on_scalar, out, window, offsets):
            if on_scalar:
                nc.scalar.activation(out=out, in_=window[:].indirect(offsets), func=ACT.Copy)
            else:
                nc.vector.tensor_copy(out, window[:].indirect(offsets))

        for t in range(PACK):
            for h in range(2):
                copy = nc.vector.tensor_copy if (t, h) in Y_DVE else nc.scalar.copy
                copy(y[t][:, halves[h]], y_bank[t][h][:])
        for t in range(PACK):
            for h in range(2):
                fetch((t, h) in A_ACT, y_n1[t][:, halves[h]], y[t], entries(l_n1, h * HALF, HALF))
            for h in range(2):
                if (t, h) in SUB_POOL:
                    nc.gpsimd.tensor_tensor(st[t][:, halves[h]], y_n1[t][:, halves[h]], y[t][:, halves[h]], ALU.subtract)
                else:
                    nc.vector.tensor_tensor(st[t][:, halves[h]], y_n1[t][:, halves[h]], y_bank[t][h][:], ALU.subtract)
        for t in range(PACK):
            for h in range(2):
                nc.scalar.activation(out=sig[t][h][:], in_=st[t][:].indirect(entries(l_n2, h * HALF, HALF)), func=ACT.Sigmoid)
        w2_plane = sb.tile([P, N], U8, name="w2_plane", align_bytes=64)
        w2_codes = sb.tile([P, N], U32, name="w2_codes", align_bytes=64)
        for dealt, raw in ((w2_codes, w2_raw_words), (w2_plane, w2_raw_bytes)):
            nc.gpsimd.tensor_copy(dealt[:].rearrange("p (t m) -> p t m", t=PACK), raw[:].rearrange("p (m t) -> p t m", t=PACK))
        nc.scalar.activation(out=warm[:, 1:2], in_=sig[3][1][:, 0:1], func=ACT.Abs_reciprocal_sqrt)

        def interleave(copy, grouped, planes):
            copy(grouped[:].rearrange("p (c i t) -> p c t i", i=4, t=PACK), planes.rearrange("p t (c i) -> p c t i", i=4))

        def make_z(h):
            for t in range(PACK):
                nc.vector.scalar_tensor_tensor(
                    out=z[h][:, t, :], in0=y_bank[t][h][:], scalar=gain[:, t : t + 1],
                    in1=sig[t][h][:], op0=ALU.mult, op1=ALU.mult,
                )

        def group_z(h, start, width):
            grouped = sb.tile([P, PACK * width], BF16, name=f"z_grouped{h}_{start}", tag=f"z_grouped{h}_{start}", align_bytes=64)
            interleave(nc.vector.tensor_copy, grouped, z[h][:, :, start : start + width])
            return grouped

        def quantise_z(grouped, h, start, width):
            codes = sb.tile([P, width], U32, name=f"z_codes{h}_{start}", align_bytes=64)
            plane = sb.tile([P, width], U8, name=f"z_plane{h}_{start}", align_bytes=64)
            nc.vector.quantize_mx(out=codes[:].bitcast(FP8X4), scales=plane[:], in_=grouped[:])
            return codes, plane, slice(start, start + width)

        def second_product(banks, pieces):
            for t in range(PACK):
                cols = slice(P * t, P * (t + 1))
                for codes, plane, where in pieces:
                    nc.tensor.matmul_mx(
                        out=banks[t][:, where], lhsT=w2_codes[:, cols].bitcast(FP8X4), lhsT_scale=w2_plane[:, cols],
                        rhs=codes[:].bitcast(FP8X4), rhs_scale=plane[:], start=True, stop=True,
                    )

        hw = [sb.tile([P, S], F32, name=f"h{t}") for t in range(PACK)]
        hh = []
        h_first = [ps.tile([P, HALF], F32, name=f"h_first{t}", tag=f"bank{t}_0") for t in range(PACK)]
        make_z(0)
        second_product(h_first, [quantise_z(group_z(0, 0, HALF), 0, 0, HALF)])
        make_z(1)
        h_second = [ps.tile([P, HALF], F32, name=f"h_second{t}", tag=f"bank{t}_1") for t in range(PACK)]
        z_last = [group_z(1, start, CHUNK) for start in (0, CHUNK)]
        second_product(h_second, [quantise_z(z_last[i], 1, i * CHUNK, CHUNK) for i in range(2)])
        h_bank = [h_first, h_second]
        for h in range(2):
            for t in range(PACK):
                copy = nc.vector.tensor_copy if (t, h) in C_DVE else nc.scalar.copy
                copy(hw[t][:, halves[h]], h_bank[h][t][:])

        out_rows = out_0.rearrange("(p t) c -> p t c", t=PACK)
        out_codes = sb.tile([P, S], U32, name="out_codes", align_bytes=64)
        out_plane = sb.tile([P, S], U8, name="out_plane", align_bytes=64)
        out_words = words_of(out_1)
        chunks = range(len(PIECES))
        pp = [sb.tile([P, PACK, PIECES[c][1]], F32, name=f"pp{c}", tag=f"pp{c}") for c in chunks]
        prod = [sb.tile([P, PACK, HALF], F32, name=f"prod{h}") for h in range(2)]
        den = [sb.tile([P, PACK, PIECES[c][1]], F32, name=f"den{c}") for c in chunks]
        root = [sb.tile([P, PACK, PIECES[c][1]], F32, name=f"root{c}", tag=f"root{c}", align_bytes=64) for c in chunks]
        inv = [sb.tile([P, PACK, PIECES[c][1]], F32, name=f"inv{c}") for c in chunks]
        pa = []
        res = {}

        def columns(c):
            return slice(PIECES[c][0], PIECES[c][0] + PIECES[c][1])

        def inner(c):
            return slice(PIECES[c][0] % HALF, PIECES[c][0] % HALF + PIECES[c][1])

        def square_h(h):
            hh.append(sb.tile([P, PACK, HALF], F32, name=f"hh{h}", tag=HH_TAG[h], align_bytes=64))
            for t in range(PACK):
                if (t, h) in HH_POOL:
                    nc.gpsimd.tensor_tensor(hh[h][:, t, :], hw[t][:, halves[h]], hw[t][:, halves[h]], ALU.mult)
                elif (t, h) in HH_DVE:
                    nc.vector.tensor_tensor(hh[h][:, t, :], hw[t][:, halves[h]], h_bank[h][t][:], ALU.mult)
                else:
                    nc.scalar.activation(out=hh[h][:, t, :], in_=h_bank[h][t][:], func=ACT.Square)

        def fetch_pa(h):
            pa.append(sb.tile([P, PACK, HALF], F32, name=f"pa{h}", tag="pp0" if h else "pa0"))
            for t in range(PACK):
                fetch((t, h) in B_ACT, pa[h][:, t, :], hw[t], entries(l_n3, h * HALF, HALF))

        def denominator(c):
            h = PIECES[c][0] // HALF
            nc.scalar.activation(out=pp[c][:], in_=pa[h][:, :, inner(c)], func=ACT.Square)
            nc.vector.tensor_tensor(den[c][:], pp[c][:], hh[h][:, :, inner(c)], ALU.add)

        def numerator(h):
            for t in range(PACK):
                nc.vector.tensor_tensor(prod[h][:, t, :], pa[h][:, t, :], h_bank[h][t][:], ALU.mult)

        def inverse_root(c):
            nc.scalar.activation(out=root[c][:], in_=den[c][:], func=ACT.Abs_reciprocal_sqrt, scale=0.5, bias=0.25)

        def invert(c):
            nc.scalar.activation(out=inv[c][:], in_=root[c][:], func=ACT.Square)

        def finish(c):
            res[c] = sb.tile([P, PACK, PIECES[c][1]], F32, name=f"res{c}", tag=f"pp{c + 2}" if c < 2 else f"res{c}")
            nc.vector.tensor_tensor(res[c][:], prod[PIECES[c][0] // HALF][:, :, inner(c)], inv[c][:], ALU.mult)
            nc.sync.dma_start(out_rows[:, :, columns(c)], res[c][:])

        def planes(c):
            grouped = sb.tile([P, PACK * PIECES[c][1]], BF16, name=f"grouped{c}", tag="root3" if c == 1 else f"grouped{c}", align_bytes=64)
            interleave(nc.scalar.copy if c in IL_ACT else nc.vector.tensor_copy, grouped, res[c][:])
            nc.vector.quantize_mx(out=out_codes[:, columns(c)].bitcast(FP8X4), scales=out_plane[:, columns(c)], in_=grouped[:])
            if columns(c).stop % HALF == 0:
                half = halves[PIECES[c][0] // HALF]
                nc.scalar.dma_start(out_words[:, half], out_codes[:, half].bitcast(I32))

        square_h(0)
        fetch_pa(0)
        denominator(0)
        denominator(1)
        numerator(0)
        square_h(1)
        fetch_pa(1)
        inverse_root(0)
        inverse_root(1)
        invert(0)
        denominator(2)
        denominator(3)
        invert(1)
        inverse_root(2)
        inverse_root(3)
        invert(2)
        invert(3)
        numerator(1)
        finish(0)
        finish(1)
        finish(2)
        finish(3)
        planes(0)
        planes(1)
        planes(2)
        planes(3)
        for q in range(4):
            queue = nc.scalar if q % 2 else nc.sync
            queue.dma_start(out_2[0, 4 * q : 4 * q + 4, :].bitcast(I32), out_plane[32 * q : 32 * q + 4, :].bitcast(I32))
